import numpy as np
CORES = [89,94,345,350]
N = 4
TK, LAY = 512, 2
def setup_inputs(rng):
    return {"x": rng.standard_normal((N, 128, TK), dtype=np.float32), "w": (rng.standard_normal((N, 128, LAY * 256), dtype=np.float32) / 16)}
def setup_inputs_big(rng):
    d = setup_inputs(rng)
    for k in ("x", "w"): d[k] = (d[k].astype(np.float32) * 1024.0).astype(d[k].dtype)
    return d
def setup_inputs_small(rng):
    d = setup_inputs(rng)
    for k in ("x", "w"): d[k] = (d[k].astype(np.float32) * (1 / 1024.0)).astype(d[k].dtype)
    return d
def setup_inputs_apart(rng):
    d = setup_inputs(rng)
    f = (10.0 ** rng.permutation(np.linspace(-1.5, 1.5, N))).astype(np.float32).reshape(N, 1, 1)
    for k in ("x", "w"): d[k] = (d[k].astype(np.float32) * f).astype(d[k].dtype)
    return d
def reference(x, w):
    X, W = x.astype(np.float64), w.astype(np.float64)
    h = list(X)
    for l in range(LAY):
        h = [np.maximum(W[r][:, 256 * l:256 * l + 128].T @ h[r] + W[r][:, 256 * l + 128:256 * l + 256].T @ h[r ^ (1 << l)], 0.0) for r in range(N)]
    return {"y": np.stack(h).astype(np.float32)}

@@ -1,0 +1,164 @@
+from concourse.bass import DstId, RemoteDMATransfer
+from concourse.mybir import AluOpType
+
+WORLD = 512
+N, TK = 4, 512
+CHUNKS = [256, 256]
+NR = 2
+RELAY_ENGINES = 4
+
+BLK, SL = [], []
+_c = 0
+for _w in CHUNKS:
+    BLK.append((_c, _c + _w))
+    for _j in range(NR):
+        SL.append((_c + _j * (_w // NR), _c + (_j + 1) * (_w // NR)))
+    _c += _w
+NT, NS = len(BLK), len(SL)
+ZW = max(b - a for a, b in SL)
+
+SCRATCH = {
+    "xs": ("sbuf", [128, TK], "float32"),
+    "ws": ("sbuf", [128, TK], "float32"),
+    "xp": ("sbuf", [128, TK], "float32"),
+    "h1": ("sbuf", [128, TK], "float32"),
+    "hp": ("sbuf", [128, TK], "float32"),
+    "yo": ("sbuf", [128, TK], "float32"),
+    "zz": ("sbuf", [128, ZW], "float32"),
+}
+for _s in range(NS):
+    SCRATCH["pa%d" % _s] = ("psum", [128, 512], "float32")
+    SCRATCH["pb%d" % _s] = ("psum", [128, 512], "float32")
+
+SEMAPHORES = (["lw0", "lw1", "zf", "sent", "st"]
+              + ["lx%d" % t for t in range(NT)] + ["xa%d" % t for t in range(NT)]
+              + [n + str(s) for s in range(NS) for n in ("ma", "ra", "ha", "mb", "rb")])
+
+
+def _bits(mask):
+    return [1 << i for i in range(mask.bit_length()) if (mask >> i) & 1]
+
+
+def _join(bits):
+    m = 0
+    for b in bits:
+        m |= b
+    return m
+
+
+def _relays(T, topo, r):
+    s, d = T.cores[r], T.cores[r ^ 2]
+    by_host = {}
+    for c in range(WORLD):
+        if T.rank_of(c) is not None or topo.host(c) in (topo.host(s), topo.host(d)):
+            continue
+        if topo.chip(c) != topo.chip(s) or topo.chip(c) != topo.chip(d):
+            continue
+        if topo.die(c) != topo.die(s) or topo.die(c) != topo.die(d):
+            continue
+        if topo.may_write(s, c) and topo.may_write(c, d):
+            by_host.setdefault(topo.host(c), []).append(c)
+    k = 0 if r < (r ^ 2) else 1
+    return [by_host[h][k] for h in sorted(by_host)][:NR]
+
+
+def _send_masks(topo, s, relays):
+    m = topo.mask(s, relays[0])
+    for c in relays[1:]:
+        m &= topo.mask(s, c)
+    bits = _bits(m)
+    return [bits[j::len(relays)] for j in range(len(relays))]
+
+
+def _relay_program(g, core, T, topo, r, j, n_in):
+    d = T.cores[r ^ 2]
+    rid, pid = topo.addr(d, core)
+    bits = _bits(topo.mask(core, d))
+    bits = bits[::len(bits) // RELAY_ENGINES][:RELAY_ENGINES]
+    for t in range(NT):
+        s = t * NR + j
+        a, b = SL[s]
+        g.wait_ge(T.sem["ha%d" % s], n_in)
+        g.remote_dma(out_ap=T.hp[:, a:b], in_ap=T.hp[:, a:b], remote_sem=T.sem["ha%d" % s], local_sem=T.sem.sent,
+                     pid=pid, routing_id=rid, dma_engine_mask=_join(bits))
+    g.wait_ge(T.sem.sent, NT * len(bits))
+
+
+def rank_program(g, core, T, topo):
+    sem = T.sem
+    rank = T.rank_of(core)
+    if rank is None:
+        for r in range(N):
+            rel = _relays(T, topo, r)
+            if core in rel:
+                j = rel.index(core)
+                _relay_program(g, core, T, topo, r, j, len(_send_masks(topo, T.cores[r], rel)[j]))
+        return
+
+    q = [g.sync, g.scalar]
+    u0, v0, u1, v1 = (T.ws[:, 128 * i:128 * (i + 1)] for i in range(4))
+    near = T.cores[rank ^ 1]
+    rel = _relays(T, topo, rank)
+    way = _send_masks(topo, core, rel)
+    ex = [b for w in way for b in w if b & topo.mask(core, near)]
+
+    for t, (a, b) in enumerate(BLK):
+        q[t % 2].dma_start(T.xs[:, a:b], T.x[:, a:b]).then_inc(sem["lx%d" % t], 16)
+    g.sync.dma_start(T.ws[:, 0:256], T.w[:, 0:256]).then_inc(sem.lw0, 16)
+    g.scalar.dma_start(T.ws[:, 256:512], T.w[:, 256:512]).then_inc(sem.lw1, 16)
+
+    sent = 0
+    rid, pid = topo.addr(near, core)
+    for t, (a, b) in enumerate(BLK):
+        g.wait_ge(sem["lx%d" % t], 16)
+        g.remote_dma(out_ap=T.xp[:, a:b], in_ap=T.xs[:, a:b], remote_sem=sem["xa%d" % t], local_sem=sem.sent,
+                     pid=pid, routing_id=rid, dma_engine_mask=_join(ex))
+        sent += len(ex)
+    for t in range(NT):
+        trs = []
+        for j, c in enumerate(rel):
+            s = t * NR + j
+            a, b = SL[s]
+            g.wait_ge(sem["ra%d" % s], 1)
+            rid, pid = topo.addr(c, core)
+            trs.append(RemoteDMATransfer(dst_ids=[DstId(rid=rid, pnc=pid)], dma_engine_mask=_join(way[j]),
+                                         remote_sem=sem["ha%d" % s], src=T.h1[:, a:b], dst=T.hp[:, a:b]))
+            sent += len(way[j])
+        g.remote_dma_fused(trs, local_sem=sem.sent)
+
+    te = g.tensor
+    te.wait_ge(sem.lw0, 16)
+    for t in range(NT):
+        te.wait_ge(sem["lx%d" % t], 16)
+        for s in range(t * NR, (t + 1) * NR):
+            a, b = SL[s]
+            te.matmul(T["pa%d" % s][:, 0:b - a], u0, T.xs[:, a:b], True, False)
+    for t in range(NT):
+        te.wait_ge(sem["xa%d" % t], len(ex))
+        for s in range(t * NR, (t + 1) * NR):
+            a, b = SL[s]
+            te.matmul(T["pa%d" % s][:, 0:b - a], v0, T.xp[:, a:b], False, True).then_inc(sem["ma%d" % s], 1)
+    te.wait_ge(sem.lw1, 16)
+    for s, (a, b) in enumerate(SL):
+        te.wait_ge(sem["ra%d" % s], 1)
+        te.matmul(T["pb%d" % s][:, 0:b - a], u1, T.h1[:, a:b], True, False)
+    for s, (a, b) in enumerate(SL):
+        te.wait_ge(sem["ha%d" % s], RELAY_ENGINES)
+        te.matmul(T["pb%d" % s][:, 0:b - a], v1, T.hp[:, a:b], False, True).then_inc(sem["mb%d" % s], 1)
+
+    ve = g.vector
+    ve.memset(T.zz[:], 0.0).then_inc(sem.zf, 1)
+    ve.wait_ge(sem.zf, 1)
+    for s, (a, b) in enumerate(SL):
+        ve.wait_ge(sem["ma%d" % s], 1)
+        ve.tensor_tensor(T.h1[:, a:b], T["pa%d" % s][:, 0:b - a], T.zz[:, 0:b - a], AluOpType.max).then_inc(sem["ra%d" % s], 1)
+    for s, (a, b) in enumerate(SL):
+        ve.wait_ge(sem["mb%d" % s], 1)
+        ve.tensor_tensor(T.yo[:, a:b], T["pb%d" % s][:, 0:b - a], T.zz[:, 0:b - a], AluOpType.max).then_inc(sem["rb%d" % s], 1)
+
+    for s, (a, b) in enumerate(SL):
+        q[s % 2].wait_ge(sem["rb%d" % s], 1)
+        q[s % 2].dma_start(T.y[:, a:b], T.yo[:, a:b]).then_inc(sem.st, 16)
+
+    g.wait_ge(sem.sent, sent)
+    g.wait_ge(sem.st, 16 * NS)

@@ -3,19 +3,16 @@ from concourse.mybir import AluOpType
 
 WORLD = 512
 N, TK = 4, 512
-CHUNKS = [256, 256]
+CHUNKS = [128, 192, 192]
 NR = 2
-RELAY_ENGINES = 4
 
 BLK, SL = [], []
 _c = 0
 for _w in CHUNKS:
     BLK.append((_c, _c + _w))
-    for _j in range(NR):
-        SL.append((_c + _j * (_w // NR), _c + (_j + 1) * (_w // NR)))
+    SL.append([(_c + _j * (_w // NR), _c + (_j + 1) * (_w // NR)) for _j in range(NR)])
     _c += _w
-NT, NS = len(BLK), len(SL)
-ZW = max(b - a for a, b in SL)
+NT = len(BLK)
 
 SCRATCH = {
     "xs": ("sbuf", [128, TK], "float32"),
@@ -24,15 +21,14 @@ SCRATCH = {
     "h1": ("sbuf", [128, TK], "float32"),
     "hp": ("sbuf", [128, TK], "float32"),
     "yo": ("sbuf", [128, TK], "float32"),
-    "zz": ("sbuf", [128, ZW], "float32"),
+    "zz": ("sbuf", [128, max(CHUNKS)], "float32"),
 }
-for _s in range(NS):
-    SCRATCH["pa%d" % _s] = ("psum", [128, 512], "float32")
-    SCRATCH["pb%d" % _s] = ("psum", [128, 512], "float32")
+for _t in range(NT):
+    SCRATCH["pa%d" % _t] = ("psum", [128, 512], "float32")
+    SCRATCH["pb%d" % _t] = ("psum", [128, 512], "float32")
 
 SEMAPHORES = (["lw0", "lw1", "zf", "sent", "st"]
-              + ["lx%d" % t for t in range(NT)] + ["xa%d" % t for t in range(NT)]
-              + [n + str(s) for s in range(NS) for n in ("ma", "ra", "ha", "mb", "rb")])
+              + [n + str(t) for t in range(NT) for n in ("lx", "xa", "ma", "ra", "ha", "mb", "rb")])
 
 
 def _bits(mask):
@@ -73,15 +69,13 @@ def _send_masks(topo, s, relays):
 def _relay_program(g, core, T, topo, r, j, n_in):
     d = T.cores[r ^ 2]
     rid, pid = topo.addr(d, core)
-    bits = _bits(topo.mask(core, d))
-    bits = bits[::len(bits) // RELAY_ENGINES][:RELAY_ENGINES]
+    m = topo.mask(core, d)
     for t in range(NT):
-        s = t * NR + j
-        a, b = SL[s]
-        g.wait_ge(T.sem["ha%d" % s], n_in)
-        g.remote_dma(out_ap=T.hp[:, a:b], in_ap=T.hp[:, a:b], remote_sem=T.sem["ha%d" % s], local_sem=T.sem.sent,
-                     pid=pid, routing_id=rid, dma_engine_mask=_join(bits))
-    g.wait_ge(T.sem.sent, NT * len(bits))
+        a, b = SL[t][j]
+        g.wait_ge(T.sem["ha%d" % t], n_in)
+        g.remote_dma(out_ap=T.hp[:, a:b], in_ap=T.hp[:, a:b], remote_sem=T.sem["ha%d" % t], local_sem=T.sem.sent,
+                     pid=pid, routing_id=rid, dma_engine_mask=m)
+    g.wait_ge(T.sem.sent, NT * len(_bits(m)))
 
 
 def rank_program(g, core, T, topo):
@@ -101,11 +95,12 @@ def rank_program(g, core, T, topo):
     rel = _relays(T, topo, rank)
     way = _send_masks(topo, core, rel)
     ex = [b for w in way for b in w if b & topo.mask(core, near)]
+    landed = sum(len(_bits(topo.mask(c, core))) for c in _relays(T, topo, rank ^ 2))
 
     for t, (a, b) in enumerate(BLK):
         q[t % 2].dma_start(T.xs[:, a:b], T.x[:, a:b]).then_inc(sem["lx%d" % t], 16)
-    g.sync.dma_start(T.ws[:, 0:256], T.w[:, 0:256]).then_inc(sem.lw0, 16)
-    g.scalar.dma_start(T.ws[:, 256:512], T.w[:, 256:512]).then_inc(sem.lw1, 16)
+    q[NT % 2].dma_start(T.ws[:, 0:256], T.w[:, 0:256]).then_inc(sem.lw0, 16)
+    q[(NT + 1) % 2].dma_start(T.ws[:, 256:512], T.w[:, 256:512]).then_inc(sem.lw1, 16)
 
     sent = 0
     rid, pid = topo.addr(near, core)
@@ -115,50 +110,45 @@ def rank_program(g, core, T, topo):
                      pid=pid, routing_id=rid, dma_engine_mask=_join(ex))
         sent += len(ex)
     for t in range(NT):
+        g.wait_ge(sem["ra%d" % t], 1)
         trs = []
         for j, c in enumerate(rel):
-            s = t * NR + j
-            a, b = SL[s]
-            g.wait_ge(sem["ra%d" % s], 1)
+            a, b = SL[t][j]
             rid, pid = topo.addr(c, core)
             trs.append(RemoteDMATransfer(dst_ids=[DstId(rid=rid, pnc=pid)], dma_engine_mask=_join(way[j]),
-                                         remote_sem=sem["ha%d" % s], src=T.h1[:, a:b], dst=T.hp[:, a:b]))
+                                         remote_sem=sem["ha%d" % t], src=T.h1[:, a:b], dst=T.hp[:, a:b]))
             sent += len(way[j])
         g.remote_dma_fused(trs, local_sem=sem.sent)
 
     te = g.tensor
     te.wait_ge(sem.lw0, 16)
-    for t in range(NT):
+    for t, (a, b) in enumerate(BLK):
         te.wait_ge(sem["lx%d" % t], 16)
-        for s in range(t * NR, (t + 1) * NR):
-            a, b = SL[s]
-            te.matmul(T["pa%d" % s][:, 0:b - a], u0, T.xs[:, a:b], True, False)
-    for t in range(NT):
+        te.matmul(T["pa%d" % t][:, 0:b - a], u0, T.xs[:, a:b], True, False)
+    for t, (a, b) in enumerate(BLK):
         te.wait_ge(sem["xa%d" % t], len(ex))
-        for s in range(t * NR, (t + 1) * NR):
-            a, b = SL[s]
-            te.matmul(T["pa%d" % s][:, 0:b - a], v0, T.xp[:, a:b], False, True).then_inc(sem["ma%d" % s], 1)
+        te.matmul(T["pa%d" % t][:, 0:b - a], v0, T.xp[:, a:b], False, True).then_inc(sem["ma%d" % t], 1)
     te.wait_ge(sem.lw1, 16)
-    for s, (a, b) in enumerate(SL):
-        te.wait_ge(sem["ra%d" % s], 1)
-        te.matmul(T["pb%d" % s][:, 0:b - a], u1, T.h1[:, a:b], True, False)
-    for s, (a, b) in enumerate(SL):
-        te.wait_ge(sem["ha%d" % s], RELAY_ENGINES)
-        te.matmul(T["pb%d" % s][:, 0:b - a], v1, T.hp[:, a:b], False, True).then_inc(sem["mb%d" % s], 1)
+    for t, (a, b) in enumerate(BLK):
+        te.wait_ge(sem["ra%d" % t], 1)
+        te.matmul(T["pb%d" % t][:, 0:b - a], u1, T.h1[:, a:b], True, False)
+    for t, (a, b) in enumerate(BLK):
+        te.wait_ge(sem["ha%d" % t], landed)
+        te.matmul(T["pb%d" % t][:, 0:b - a], v1, T.hp[:, a:b], False, True).then_inc(sem["mb%d" % t], 1)
 
     ve = g.vector
     ve.memset(T.zz[:], 0.0).then_inc(sem.zf, 1)
     ve.wait_ge(sem.zf, 1)
-    for s, (a, b) in enumerate(SL):
-        ve.wait_ge(sem["ma%d" % s], 1)
-        ve.tensor_tensor(T.h1[:, a:b], T["pa%d" % s][:, 0:b - a], T.zz[:, 0:b - a], AluOpType.max).then_inc(sem["ra%d" % s], 1)
-    for s, (a, b) in enumerate(SL):
-        ve.wait_ge(sem["mb%d" % s], 1)
-        ve.tensor_tensor(T.yo[:, a:b], T["pb%d" % s][:, 0:b - a], T.zz[:, 0:b - a], AluOpType.max).then_inc(sem["rb%d" % s], 1)
+    for t, (a, b) in enumerate(BLK):
+        ve.wait_ge(sem["ma%d" % t], 1)
+        ve.tensor_tensor(T.h1[:, a:b], T["pa%d" % t][:, 0:b - a], T.zz[:, 0:b - a], AluOpType.max).then_inc(sem["ra%d" % t], 1)
+    for t, (a, b) in enumerate(BLK):
+        ve.wait_ge(sem["mb%d" % t], 1)
+        ve.tensor_tensor(T.yo[:, a:b], T["pb%d" % t][:, 0:b - a], T.zz[:, 0:b - a], AluOpType.max).then_inc(sem["rb%d" % t], 1)
 
-    for s, (a, b) in enumerate(SL):
-        q[s % 2].wait_ge(sem["rb%d" % s], 1)
-        q[s % 2].dma_start(T.y[:, a:b], T.yo[:, a:b]).then_inc(sem.st, 16)
+    for t, (a, b) in enumerate(BLK):
+        q[t % 2].wait_ge(sem["rb%d" % t], 1)
+        q[t % 2].dma_start(T.y[:, a:b], T.yo[:, a:b]).then_inc(sem.st, 16)
 
     g.wait_ge(sem.sent, sent)
-    g.wait_ge(sem.st, 16 * NS)
+    g.wait_ge(sem.st, 16 * NT)

@@ -3,7 +3,7 @@ from concourse.mybir import AluOpType
 
 WORLD = 512
 N, TK = 4, 512
-CHUNKS = [128, 192, 192]
+CHUNKS = [80, 128, 152, 152]
 NR = 2
 
 BLK, SL = [], []
@@ -13,6 +13,7 @@ for _w in CHUNKS:
     SL.append([(_c + _j * (_w // NR), _c + (_j + 1) * (_w // NR)) for _j in range(NR)])
     _c += _w
 NT = len(BLK)
+NG = NT - 1 + NR
 
 SCRATCH = {
     "xs": ("sbuf", [128, TK], "float32"),
@@ -28,7 +29,9 @@ for _t in range(NT):
     SCRATCH["pb%d" % _t] = ("psum", [128, 512], "float32")
 
 SEMAPHORES = (["lw0", "lw1", "zf", "sent", "st"]
-              + [n + str(t) for t in range(NT) for n in ("lx", "xa", "ma", "ra", "ha", "mb", "rb")])
+              + [n + str(t) for t in range(NT) for n in ("lx", "xa", "ma", "ra", "ha")]
+              + ["hb%d" % j for j in range(NR)]
+              + [n + str(k) for k in range(NG) for n in ("mb", "rb")])
 
 
 def _bits(mask):
@@ -73,7 +76,8 @@ def _relay_program(g, core, T, topo, r, j, n_in):
     for t in range(NT):
         a, b = SL[t][j]
         g.wait_ge(T.sem["ha%d" % t], n_in)
-        g.remote_dma(out_ap=T.hp[:, a:b], in_ap=T.hp[:, a:b], remote_sem=T.sem["ha%d" % t], local_sem=T.sem.sent,
+        there = T.sem["ha%d" % t] if t < NT - 1 else T.sem["hb%d" % j]
+        g.remote_dma(out_ap=T.hp[:, a:b], in_ap=T.hp[:, a:b], remote_sem=there, local_sem=T.sem.sent,
                      pid=pid, routing_id=rid, dma_engine_mask=m)
     g.wait_ge(T.sem.sent, NT * len(_bits(m)))
 
@@ -89,26 +93,37 @@ def rank_program(g, core, T, topo):
                 _relay_program(g, core, T, topo, r, j, len(_send_masks(topo, T.cores[r], rel)[j]))
         return
 
-    q = [g.sync, g.scalar]
     u0, v0, u1, v1 = (T.ws[:, 128 * i:128 * (i + 1)] for i in range(4))
     near = T.cores[rank ^ 1]
     rel = _relays(T, topo, rank)
     way = _send_masks(topo, core, rel)
-    ex = [b for w in way for b in w if b & topo.mask(core, near)]
-    landed = sum(len(_bits(topo.mask(c, core))) for c in _relays(T, topo, rank ^ 2))
+    out = [b for w in way for b in w]
+    ex = [[b for b in _bits(topo.mask(core, near)) if b in out],
+          [b for b in _bits(topo.mask(core, near)) if b not in out]]
+    per = [len(_bits(topo.mask(c, core))) for c in _relays(T, topo, rank ^ 2)]
 
-    for t, (a, b) in enumerate(BLK):
-        q[t % 2].dma_start(T.xs[:, a:b], T.x[:, a:b]).then_inc(sem["lx%d" % t], 16)
-    q[NT % 2].dma_start(T.ws[:, 0:256], T.w[:, 0:256]).then_inc(sem.lw0, 16)
-    q[(NT + 1) % 2].dma_start(T.ws[:, 256:512], T.w[:, 256:512]).then_inc(sem.lw1, 16)
+    grp = [(t, "pb%d" % t, BLK[t][0], BLK[t][1], "ha%d" % t, sum(per)) for t in range(NT - 1)]
+    for j in range(NR):
+        grp.append((NT - 1, "pb%d" % (NT - 1) if j == 0 else "pa%d" % (j - 1), SL[NT - 1][j][0], SL[NT - 1][j][1],
+                    "hb%d" % j, per[j]))
+
+    def load_x(qq, t):
+        a, b = BLK[t]
+        qq.dma_start(T.xs[:, a:b], T.x[:, a:b]).then_inc(sem["lx%d" % t], 16)
+    load_x(g.sync, 0)
+    load_x(g.scalar, 1)
+    g.sync.dma_start(T.ws[:, 0:256], T.w[:, 0:256]).then_inc(sem.lw0, 16)
+    load_x(g.scalar, 2)
+    load_x(g.sync, 3)
+    g.scalar.dma_start(T.ws[:, 256:512], T.w[:, 256:512]).then_inc(sem.lw1, 16)
 
     sent = 0
     rid, pid = topo.addr(near, core)
     for t, (a, b) in enumerate(BLK):
         g.wait_ge(sem["lx%d" % t], 16)
         g.remote_dma(out_ap=T.xp[:, a:b], in_ap=T.xs[:, a:b], remote_sem=sem["xa%d" % t], local_sem=sem.sent,
-                     pid=pid, routing_id=rid, dma_engine_mask=_join(ex))
-        sent += len(ex)
+                     pid=pid, routing_id=rid, dma_engine_mask=_join(ex[t % 2]))
+        sent += len(ex[t % 2])
     for t in range(NT):
         g.wait_ge(sem["ra%d" % t], 1)
         trs = []
@@ -126,15 +141,15 @@ def rank_program(g, core, T, topo):
         te.wait_ge(sem["lx%d" % t], 16)
         te.matmul(T["pa%d" % t][:, 0:b - a], u0, T.xs[:, a:b], True, False)
     for t, (a, b) in enumerate(BLK):
-        te.wait_ge(sem["xa%d" % t], len(ex))
+        te.wait_ge(sem["xa%d" % t], len(ex[t % 2]))
         te.matmul(T["pa%d" % t][:, 0:b - a], v0, T.xp[:, a:b], False, True).then_inc(sem["ma%d" % t], 1)
     te.wait_ge(sem.lw1, 16)
-    for t, (a, b) in enumerate(BLK):
+    for t, bank, a, b, arr, cnt in grp:
         te.wait_ge(sem["ra%d" % t], 1)
-        te.matmul(T["pb%d" % t][:, 0:b - a], u1, T.h1[:, a:b], True, False)
-    for t, (a, b) in enumerate(BLK):
-        te.wait_ge(sem["ha%d" % t], landed)
-        te.matmul(T["pb%d" % t][:, 0:b - a], v1, T.hp[:, a:b], False, True).then_inc(sem["mb%d" % t], 1)
+        te.matmul(T[bank][:, 0:b - a], u1, T.h1[:, a:b], True, False)
+    for k, (t, bank, a, b, arr, cnt) in enumerate(grp):
+        te.wait_ge(sem[arr], cnt)
+        te.matmul(T[bank][:, 0:b - a], v1, T.hp[:, a:b], False, True).then_inc(sem["mb%d" % k], 1)
 
     ve = g.vector
     ve.memset(T.zz[:], 0.0).then_inc(sem.zf, 1)
@@ -142,13 +157,14 @@ def rank_program(g, core, T, topo):
     for t, (a, b) in enumerate(BLK):
         ve.wait_ge(sem["ma%d" % t], 1)
         ve.tensor_tensor(T.h1[:, a:b], T["pa%d" % t][:, 0:b - a], T.zz[:, 0:b - a], AluOpType.max).then_inc(sem["ra%d" % t], 1)
-    for t, (a, b) in enumerate(BLK):
-        ve.wait_ge(sem["mb%d" % t], 1)
-        ve.tensor_tensor(T.yo[:, a:b], T["pb%d" % t][:, 0:b - a], T.zz[:, 0:b - a], AluOpType.max).then_inc(sem["rb%d" % t], 1)
+    for k, (t, bank, a, b, arr, cnt) in enumerate(grp):
+        ve.wait_ge(sem["mb%d" % k], 1)
+        ve.tensor_tensor(T.yo[:, a:b], T[bank][:, 0:b - a], T.zz[:, 0:b - a], AluOpType.max).then_inc(sem["rb%d" % k], 1)
 
-    for t, (a, b) in enumerate(BLK):
-        q[t % 2].wait_ge(sem["rb%d" % t], 1)
-        q[t % 2].dma_start(T.y[:, a:b], T.yo[:, a:b]).then_inc(sem.st, 16)
+    q = [g.sync, g.scalar]
+    for k, (t, bank, a, b, arr, cnt) in enumerate(grp):
+        q[k % 2].wait_ge(sem["rb%d" % k], 1)
+        q[k % 2].dma_start(T.y[:, a:b], T.yo[:, a:b]).then_inc(sem.st, 16)
 
     g.wait_ge(sem.sent, sent)
-    g.wait_ge(sem.st, 16 * NT)
+    g.wait_ge(sem.st, 16 * NG)

@@ -5,6 +5,7 @@ WORLD = 512
 N, TK = 4, 512
 CHUNKS = [80, 128, 152, 152]
 NR = 2
+NQ = 2
 
 BLK, SL = [], []
 _c = 0
@@ -58,28 +59,30 @@ def _relays(T, topo, r):
         if topo.may_write(s, c) and topo.may_write(c, d):
             by_host.setdefault(topo.host(c), []).append(c)
     k = 0 if r < (r ^ 2) else 1
-    return [by_host[h][k] for h in sorted(by_host)][:NR]
+    return [by_host[h][k::2][:NQ] for h in sorted(by_host)][:NR]
 
 
 def _send_masks(topo, s, relays):
-    m = topo.mask(s, relays[0])
-    for c in relays[1:]:
-        m &= topo.mask(s, c)
+    m = topo.mask(s, relays[0][0])
+    for w in relays:
+        for c in w:
+            m &= topo.mask(s, c)
     bits = _bits(m)
     return [bits[j::len(relays)] for j in range(len(relays))]
 
 
-def _relay_program(g, core, T, topo, r, j, n_in):
+def _relay_program(g, core, T, topo, r, j, i, n_in):
     d = T.cores[r ^ 2]
     rid, pid = topo.addr(d, core)
     m = topo.mask(core, d)
-    for t in range(NT):
+    mine = [t for t in range(NT) if t % NQ == i]
+    for t in mine:
         a, b = SL[t][j]
         g.wait_ge(T.sem["ha%d" % t], n_in)
         there = T.sem["ha%d" % t] if t < NT - 1 else T.sem["hb%d" % j]
         g.remote_dma(out_ap=T.hp[:, a:b], in_ap=T.hp[:, a:b], remote_sem=there, local_sem=T.sem.sent,
                      pid=pid, routing_id=rid, dma_engine_mask=m)
-    g.wait_ge(T.sem.sent, NT * len(_bits(m)))
+    g.wait_ge(T.sem.sent, len(mine) * len(_bits(m)))
 
 
 def rank_program(g, core, T, topo):
@@ -88,9 +91,9 @@ def rank_program(g, core, T, topo):
     if rank is None:
         for r in range(N):
             rel = _relays(T, topo, r)
-            if core in rel:
-                j = rel.index(core)
-                _relay_program(g, core, T, topo, r, j, len(_send_masks(topo, T.cores[r], rel)[j]))
+            for j, w in enumerate(rel):
+                if core in w:
+                    _relay_program(g, core, T, topo, r, j, w.index(core), len(_send_masks(topo, T.cores[r], rel)[j]))
         return
 
     u0, v0, u1, v1 = (T.ws[:, 128 * i:128 * (i + 1)] for i in range(4))
@@ -100,7 +103,7 @@ def rank_program(g, core, T, topo):
     out = [b for w in way for b in w]
     ex = [[b for b in _bits(topo.mask(core, near)) if b in out],
           [b for b in _bits(topo.mask(core, near)) if b not in out]]
-    per = [len(_bits(topo.mask(c, core))) for c in _relays(T, topo, rank ^ 2)]
+    per = [len(_bits(topo.mask(w[0], core))) for w in _relays(T, topo, rank ^ 2)]
 
     grp = [(t, "pb%d" % t, BLK[t][0], BLK[t][1], "ha%d" % t, sum(per)) for t in range(NT - 1)]
     for j in range(NR):
@@ -127,9 +130,9 @@ def rank_program(g, core, T, topo):
     for t in range(NT):
         g.wait_ge(sem["ra%d" % t], 1)
         trs = []
-        for j, c in enumerate(rel):
+        for j, w in enumerate(rel):
             a, b = SL[t][j]
-            rid, pid = topo.addr(c, core)
+            rid, pid = topo.addr(w[t % NQ], core)
             trs.append(RemoteDMATransfer(dst_ids=[DstId(rid=rid, pnc=pid)], dma_engine_mask=_join(way[j]),
                                          remote_sem=sem["ha%d" % t], src=T.h1[:, a:b], dst=T.hp[:, a:b]))
             sent += len(way[j])

from concourse.bass import DstId, RemoteDMATransfer
from concourse.mybir import AluOpType

WORLD = 512
N, TK = 4, 512
CHUNKS = [80, 128, 152, 152]
NR = 2
NQ = 2

BLK, SL = [], []
_c = 0
for _w in CHUNKS:
    BLK.append((_c, _c + _w))
    SL.append([(_c + _j * (_w // NR), _c + (_j + 1) * (_w // NR)) for _j in range(NR)])
    _c += _w
NT = len(BLK)
NG = NT - 1 + NR

SCRATCH = {
    "xs": ("sbuf", [128, TK], "float32"),
    "ws": ("sbuf", [128, TK], "float32"),
    "xp": ("sbuf", [128, TK], "float32"),
    "h1": ("sbuf", [128, TK], "float32"),
    "hp": ("sbuf", [128, TK], "float32"),
    "yo": ("sbuf", [128, TK], "float32"),
    "zz": ("sbuf", [128, max(CHUNKS)], "float32"),
}
for _t in range(NT):
    SCRATCH["pa%d" % _t] = ("psum", [128, 512], "float32")
    SCRATCH["pb%d" % _t] = ("psum", [128, 512], "float32")

SEMAPHORES = (["lw0", "lw1", "zf", "sent", "st"]
              + [n + str(t) for t in range(NT) for n in ("lx", "xa", "ma", "ra", "ha")]
              + ["hb%d" % j for j in range(NR)]
              + [n + str(k) for k in range(NG) for n in ("mb", "rb")])


def _bits(mask):
    return [1 << i for i in range(mask.bit_length()) if (mask >> i) & 1]


def _join(bits):
    m = 0
    for b in bits:
        m |= b
    return m


def _relays(T, topo, r):
    s, d = T.cores[r], T.cores[r ^ 2]
    by_host = {}
    for c in range(WORLD):
        if T.rank_of(c) is not None or topo.host(c) in (topo.host(s), topo.host(d)):
            continue
        if topo.chip(c) != topo.chip(s) or topo.chip(c) != topo.chip(d):
            continue
        if topo.die(c) != topo.die(s) or topo.die(c) != topo.die(d):
            continue
        if topo.may_write(s, c) and topo.may_write(c, d):
            by_host.setdefault(topo.host(c), []).append(c)
    k = 0 if r < (r ^ 2) else 1
    return [by_host[h][k::2][:NQ] for h in sorted(by_host)][:NR]


def _send_masks(topo, s, relays):
    m = topo.mask(s, relays[0][0])
    for w in relays:
        for c in w:
            m &= topo.mask(s, c)
    bits = _bits(m)
    return [bits[j::len(relays)] for j in range(len(relays))]


def _relay_program(g, core, T, topo, r, j, i, n_in):
    d = T.cores[r ^ 2]
    rid, pid = topo.addr(d, core)
    m = topo.mask(core, d)
    mine = [t for t in range(NT) if t % NQ == i]
    for t in mine:
        a, b = SL[t][j]
        g.wait_ge(T.sem["ha%d" % t], n_in)
        there = T.sem["ha%d" % t] if t < NT - 1 else T.sem["hb%d" % j]
        g.remote_dma(out_ap=T.hp[:, a:b], in_ap=T.hp[:, a:b], remote_sem=there, local_sem=T.sem.sent,
                     pid=pid, routing_id=rid, dma_engine_mask=m)
    g.wait_ge(T.sem.sent, len(mine) * len(_bits(m)))


def rank_program(g, core, T, topo):
    sem = T.sem
    rank = T.rank_of(core)
    if rank is None:
        for r in range(N):
            rel = _relays(T, topo, r)
            for j, w in enumerate(rel):
                if core in w:
                    _relay_program(g, core, T, topo, r, j, w.index(core), len(_send_masks(topo, T.cores[r], rel)[j]))
        return

    u0, v0, u1, v1 = (T.ws[:, 128 * i:128 * (i + 1)] for i in range(4))
    near = T.cores[rank ^ 1]
    rel = _relays(T, topo, rank)
    way = _send_masks(topo, core, rel)
    out = [b for w in way for b in w]
    ex = [[b for b in _bits(topo.mask(core, near)) if b in out],
          [b for b in _bits(topo.mask(core, near)) if b not in out]]
    per = [len(_bits(topo.mask(w[0], core))) for w in _relays(T, topo, rank ^ 2)]

    grp = [(t, "pb%d" % t, BLK[t][0], BLK[t][1], "ha%d" % t, sum(per)) for t in range(NT - 1)]
    for j in range(NR):
        grp.append((NT - 1, "pb%d" % (NT - 1) if j == 0 else "pa%d" % (j - 1), SL[NT - 1][j][0], SL[NT - 1][j][1],
                    "hb%d" % j, per[j]))

    def load_x(qq, t):
        a, b = BLK[t]
        qq.dma_start(T.xs[:, a:b], T.x[:, a:b]).then_inc(sem["lx%d" % t], 16)
    load_x(g.sync, 0)
    load_x(g.scalar, 1)
    g.sync.dma_start(T.ws[:, 0:256], T.w[:, 0:256]).then_inc(sem.lw0, 16)
    load_x(g.scalar, 2)
    load_x(g.sync, 3)
    g.scalar.dma_start(T.ws[:, 256:512], T.w[:, 256:512]).then_inc(sem.lw1, 16)

    sent = 0
    rid, pid = topo.addr(near, core)
    for t, (a, b) in enumerate(BLK):
        g.wait_ge(sem["lx%d" % t], 16)
        g.remote_dma(out_ap=T.xp[:, a:b], in_ap=T.xs[:, a:b], remote_sem=sem["xa%d" % t], local_sem=sem.sent,
                     pid=pid, routing_id=rid, dma_engine_mask=_join(ex[t % 2]))
        sent += len(ex[t % 2])
    for t in range(NT):
        g.wait_ge(sem["ra%d" % t], 1)
        trs = []
        for j, w in enumerate(rel):
            a, b = SL[t][j]
            rid, pid = topo.addr(w[t % NQ], core)
            trs.append(RemoteDMATransfer(dst_ids=[DstId(rid=rid, pnc=pid)], dma_engine_mask=_join(way[j]),
                                         remote_sem=sem["ha%d" % t], src=T.h1[:, a:b], dst=T.hp[:, a:b]))
            sent += len(way[j])
        g.remote_dma_fused(trs, local_sem=sem.sent)

    te = g.tensor
    te.wait_ge(sem.lw0, 16)
    for t, (a, b) in enumerate(BLK):
        te.wait_ge(sem["lx%d" % t], 16)
        te.matmul(T["pa%d" % t][:, 0:b - a], u0, T.xs[:, a:b], True, False)
    for t, (a, b) in enumerate(BLK):
        te.wait_ge(sem["xa%d" % t], len(ex[t % 2]))
        te.matmul(T["pa%d" % t][:, 0:b - a], v0, T.xp[:, a:b], False, True).then_inc(sem["ma%d" % t], 1)
    te.wait_ge(sem.lw1, 16)
    for t, bank, a, b, arr, cnt in grp:
        te.wait_ge(sem["ra%d" % t], 1)
        te.matmul(T[bank][:, 0:b - a], u1, T.h1[:, a:b], True, False)
    for k, (t, bank, a, b, arr, cnt) in enumerate(grp):
        te.wait_ge(sem[arr], cnt)
        te.matmul(T[bank][:, 0:b - a], v1, T.hp[:, a:b], False, True).then_inc(sem["mb%d" % k], 1)

    ve = g.vector
    ve.memset(T.zz[:], 0.0).then_inc(sem.zf, 1)
    ve.wait_ge(sem.zf, 1)
    for t, (a, b) in enumerate(BLK):
        ve.wait_ge(sem["ma%d" % t], 1)
        ve.tensor_tensor(T.h1[:, a:b], T["pa%d" % t][:, 0:b - a], T.zz[:, 0:b - a], AluOpType.max).then_inc(sem["ra%d" % t], 1)
    for k, (t, bank, a, b, arr, cnt) in enumerate(grp):
        ve.wait_ge(sem["mb%d" % k], 1)
        ve.tensor_tensor(T.yo[:, a:b], T[bank][:, 0:b - a], T.zz[:, 0:b - a], AluOpType.max).then_inc(sem["rb%d" % k], 1)

    q = [g.sync, g.scalar]
    for k, (t, bank, a, b, arr, cnt) in enumerate(grp):
        q[k % 2].wait_ge(sem["rb%d" % k], 1)
        q[k % 2].dma_start(T.y[:, a:b], T.yo[:, a:b]).then_inc(sem.st, 16)

    g.wait_ge(sem.sent, sent)
    g.wait_ge(sem.st, 16 * NG)
